import numpy as np
import ml_dtypes

BF16 = ml_dtypes.bfloat16


def bf(x):
    return np.asarray(x, np.float32).astype(BF16)


def f32(x):
    return np.asarray(x, np.float32)


def f64(x):
    return np.asarray(x).astype(np.float64)


def striped(idx):
    return np.tile(idx.reshape(-1, 16).T, (8, 1))


S, K, M, N, V, F = 512, 128, 128, 768, 128, 6


def setup_inputs():
    return {"table": bf(np.random.standard_normal((F, K, S))), "w": bf(np.random.standard_normal((K, M)) / np.sqrt(F * K)), "offs": striped(np.concatenate([np.random.permutation(np.tile(np.arange(S), 2))[:V] for _ in range(F)]))}


def reference(table, w, offs):
    idx = offs[:16].T.reshape(-1)
    y = f64(w).T @ sum(f64(table)[f][:, idx[f * V : (f + 1) * V]] for f in range(F))
    return y

@@ -1,0 +1,34 @@
+import concourse.mybir as mybir
+
+BF16, F32, U16 = mybir.dt.bfloat16, mybir.dt.float32, mybir.dt.uint16
+
+CODEBOOKS, FEATURES, CODES = 6, 128, 512
+OUT_FEATURES, FRAMES = 128, 128
+LIST_COLUMNS = FRAMES // 16
+
+FLOPS = 2 * CODEBOOKS * FEATURES * OUT_FEATURES * FRAMES
+
+
+def tile_rows_fields_none_rep_kernel(tc, table, w, offs, out):
+    nc = tc.nc
+    with (
+        tc.tile_pool(name="sbuf", bufs=1) as sbuf,
+        tc.psum_pool(name="psum", bufs=1) as psum,
+    ):
+        offsets = sbuf.tile([128, CODEBOOKS * LIST_COLUMNS], U16)
+        nc.sync.dma_start(offsets[:], offs)
+        weights = sbuf.tile([FEATURES, OUT_FEATURES], BF16)
+        nc.sync.dma_start(weights[:], w)
+
+        books = [sbuf.tile([FEATURES, CODES], BF16, name=f"book{f}") for f in range(CODEBOOKS)]
+        for f in range(CODEBOOKS):
+            nc.sync.dma_start(books[f][:], table[f])
+
+        total = psum.tile([OUT_FEATURES, FRAMES], F32)
+        for f in range(CODEBOOKS):
+            picked = books[f][:].indirect(offsets[:, f * LIST_COLUMNS : (f + 1) * LIST_COLUMNS])
+            nc.tensor.matmul(total[:], weights[:], picked, start=(f == 0), stop=(f == CODEBOOKS - 1))
+
+        result = sbuf.tile([OUT_FEATURES, FRAMES], F32)
+        nc.vector.tensor_copy(result[:], total[:])
+        nc.sync.dma_start(out, result[:])

@@ -16,17 +16,17 @@ def tile_rows_fields_none_rep_kernel(tc, table, w, offs, out):
         tc.psum_pool(name="psum", bufs=1) as psum,
     ):
         offsets = sbuf.tile([128, CODEBOOKS * LIST_COLUMNS], U16)
-        nc.sync.dma_start(offsets[:], offs)
         weights = sbuf.tile([FEATURES, OUT_FEATURES], BF16)
+        nc.sync.dma_start(offsets[:], offs)
         nc.sync.dma_start(weights[:], w)
 
-        books = [sbuf.tile([FEATURES, CODES], BF16, name=f"book{f}") for f in range(CODEBOOKS)]
-        for f in range(CODEBOOKS):
-            nc.sync.dma_start(books[f][:], table[f])
+        pairs = [sbuf.tile([FEATURES, 2, CODES], BF16, name=f"pair{p}") for p in range(CODEBOOKS // 2)]
+        for p in range(CODEBOOKS // 2):
+            nc.sync.dma_start(pairs[p][:], table[2 * p : 2 * p + 2].rearrange("f k s -> k f s"))
 
         total = psum.tile([OUT_FEATURES, FRAMES], F32)
         for f in range(CODEBOOKS):
-            picked = books[f][:].indirect(offsets[:, f * LIST_COLUMNS : (f + 1) * LIST_COLUMNS])
+            picked = pairs[f // 2][:, f % 2, :].indirect(offsets[:, f * LIST_COLUMNS : (f + 1) * LIST_COLUMNS])
             nc.tensor.matmul(total[:], weights[:], picked, start=(f == 0), stop=(f == CODEBOOKS - 1))
 
         result = sbuf.tile([OUT_FEATURES, FRAMES], F32)

@@ -18,11 +18,12 @@ def tile_rows_fields_none_rep_kernel(tc, table, w, offs, out):
         offsets = sbuf.tile([128, CODEBOOKS * LIST_COLUMNS], U16)
         weights = sbuf.tile([FEATURES, OUT_FEATURES], BF16)
         nc.sync.dma_start(offsets[:], offs)
-        nc.sync.dma_start(weights[:], w)
+        nc.scalar.dma_start(weights[:], w)
 
         pairs = [sbuf.tile([FEATURES, 2, CODES], BF16, name=f"pair{p}") for p in range(CODEBOOKS // 2)]
         for p in range(CODEBOOKS // 2):
-            nc.sync.dma_start(pairs[p][:], table[2 * p : 2 * p + 2].rearrange("f k s -> k f s"))
+            queue = nc.sync if p % 2 == 0 else nc.scalar
+            queue.dma_start(pairs[p][:], table[2 * p : 2 * p + 2].rearrange("f k s -> k f s"))
 
         total = psum.tile([OUT_FEATURES, FRAMES], F32)
         for f in range(CODEBOOKS):

import concourse.mybir as mybir

BF16, F32, U16 = mybir.dt.bfloat16, mybir.dt.float32, mybir.dt.uint16

CODEBOOKS, FEATURES, CODES = 6, 128, 512
OUT_FEATURES, FRAMES = 128, 128
LIST_COLUMNS = FRAMES // 16

FLOPS = 2 * CODEBOOKS * FEATURES * OUT_FEATURES * FRAMES


def tile_rows_fields_none_rep_kernel(tc, table, w, offs, out):
    nc = tc.nc
    with (
        tc.tile_pool(name="sbuf", bufs=1) as sbuf,
        tc.psum_pool(name="psum", bufs=1) as psum,
    ):
        offsets = sbuf.tile([128, CODEBOOKS * LIST_COLUMNS], U16)
        weights = sbuf.tile([FEATURES, OUT_FEATURES], BF16)
        nc.sync.dma_start(offsets[:], offs)
        nc.scalar.dma_start(weights[:], w)

        pairs = [sbuf.tile([FEATURES, 2, CODES], BF16, name=f"pair{p}") for p in range(CODEBOOKS // 2)]
        for p in range(CODEBOOKS // 2):
            queue = nc.sync if p % 2 == 0 else nc.scalar
            queue.dma_start(pairs[p][:], table[2 * p : 2 * p + 2].rearrange("f k s -> k f s"))

        total = psum.tile([OUT_FEATURES, FRAMES], F32)
        for f in range(CODEBOOKS):
            picked = pairs[f // 2][:, f % 2, :].indirect(offsets[:, f * LIST_COLUMNS : (f + 1) * LIST_COLUMNS])
            nc.tensor.matmul(total[:], weights[:], picked, start=(f == 0), stop=(f == CODEBOOKS - 1))

        result = sbuf.tile([OUT_FEATURES, FRAMES], F32)
        nc.vector.tensor_copy(result[:], total[:])
        nc.sync.dma_start(out, result[:])
